import numpy as np
import ml_dtypes


def mxq(x, axis, fmt="e4m3"):
    dtype, down = {"e4m3": (ml_dtypes.float8_e4m3fn, 7), "e5m2": (ml_dtypes.float8_e5m2, 14)}[fmt]
    v = np.moveaxis(np.asarray(x, np.float32).astype(ml_dtypes.bfloat16).astype(np.float64), axis, -1)
    blocks = v.reshape(v.shape[:-1] + (-1, 32))
    amax = np.abs(blocks).max(-1, keepdims=True)
    byte = np.maximum(np.where(amax > 0, np.frexp(amax)[1] - 1 + 127, 0) - down, 1)
    scale = np.exp2(byte - 127.0)
    codes = (blocks / scale).astype(np.float32).astype(dtype).astype(np.float64)
    return np.moveaxis((codes * scale).reshape(v.shape), -1, axis)


WIDE = False


def mx_kscale(k):
    if not WIDE:
        return np.ones(k)
    levels = np.array([10, -10, 5, -5, 0])
    if k % 512:
        return np.exp2(np.random.permutation(np.resize(levels, k // 32))).repeat(32)
    a = np.empty((k // 512, 16))
    for p in range(k // 512):
        a[p, :8] = np.random.permutation(np.resize(levels, 8))
        for g in range(8):
            far = levels[np.abs(levels - a[p, g]) >= 10]
            a[p, g + 8] = far[np.random.randint(len(far))]
    return np.exp2(a.ravel()).repeat(32)


def f64(x):
    return np.asarray(x).astype(np.float64)


def striped(idx):
    return np.tile(idx.reshape(-1, 16).T, (8, 1)).astype(np.uint16)


def unstriped(offs):
    return offs[:16].T.reshape(-1).astype(np.int64)


def pack_weight(w):
    k, n = w.shape
    w = f64(np.asarray(w, np.float32).astype(ml_dtypes.bfloat16)).reshape(k // 32, 32, n)
    amax = np.abs(w).max(1)
    byte = np.clip(np.where(amax > 0, np.frexp(amax)[1] - 1 + 127 - 7, 1), 1, 254)
    scaled = (w * np.exp2(127.0 - byte)[:, None, :]).reshape(k, n).astype(np.float32)
    words = np.ascontiguousarray(scaled.reshape(k // 512, 128, 4, n).transpose(0, 1, 3, 2)).astype(ml_dtypes.float8_e4m3fn).view(np.uint8)
    return words, np.ascontiguousarray(byte.astype(np.uint8).reshape(k // 512, 16, n))


def unpack_weight(words, scales):
    g, p, n, _ = words.shape
    vals = np.ascontiguousarray(words).view(ml_dtypes.float8_e4m3fn).astype(np.float64) * np.repeat(np.exp2(scales.astype(np.float64) - 127.0), 8, axis=1)[..., None]
    return vals.transpose(0, 1, 3, 2).reshape(g * 512, n)


E2M1 = np.array([0.0, 0.5, 1.0, 1.5, 2.0, 3.0, 4.0, 6.0, -0.0, -0.5, -1.0, -1.5, -2.0, -3.0, -4.0, -6.0])


def pack_fp4(w):
    k, n = w.shape
    w = f64(np.asarray(w, np.float32).astype(ml_dtypes.bfloat16)).reshape(k // 32, 32, n)
    amax = np.abs(w).max(1)
    mant, ex = np.frexp(amax / 6.0)
    byte = np.clip(np.where(amax > 0, np.where(mant > 0.5, ex, ex - 1) + 127, 1), 1, 254)
    scaled = (w * np.exp2(127.0 - byte)[:, None, :]).reshape(k, n).astype(np.float32)
    c = np.ascontiguousarray(scaled.reshape(k // 512, 128, 4, n).transpose(0, 1, 3, 2)).astype(ml_dtypes.float4_e2m1fn).view(np.uint8) & 0xF
    words = (c[..., 0::2] | (c[..., 1::2] << 4)).reshape(k // 512, 128, 2 * n)
    return np.ascontiguousarray(words), np.ascontiguousarray(byte.astype(np.uint8).reshape(k // 512, 16, n))


def unpack_fp4(words, scales):
    g, _, n = scales.shape
    words = np.ascontiguousarray(words).reshape(g, 128, n, 2)
    nib = np.empty((g, 128, n, 4), np.uint8)
    nib[..., 0::2] = words & 0xF
    nib[..., 1::2] = words >> 4
    vals = E2M1[nib] * np.repeat(np.exp2(scales.astype(np.float64) - 127.0), 8, axis=1)[..., None]
    return vals.transpose(0, 1, 3, 2).reshape(g * 512, n)


def gelu(v):
    return 0.5 * v * (1.0 + np.tanh(np.sqrt(2.0 / np.pi) * (v + 0.044715 * v**3)))


K, T, S, V, H, N = 512, 2048, 1024, 512, 512, 128


def setup_inputs():
    n = np.random.standard_normal
    s = mx_kscale(K)[:, None]
    u = mx_kscale(H)
    packed_xT = pack_weight(n((K, T)) * s)
    packed_w2 = pack_fp4(n((H, N)) / np.sqrt(2 * H) / u[:, None])
    packed_w3 = pack_fp4(n((H, N)) / np.sqrt(2 * H) / u[:, None])
    return {
        "x_words": packed_xT[0],
        "x_scales": packed_xT[1],
        "w1": (n((K, H)) / np.sqrt(K) / s * u).astype(np.float32),
        "w2_words": packed_w2[0],
        "w2_scales": packed_w2[1],
        "w3_words": packed_w3[0],
        "w3_scales": packed_w3[1],
        "offs": striped(np.random.permutation(T)[:S]),
    }


def reference(x_words, x_scales, w1, w2_words, w2_scales, w3_words, w3_scales, offs):
    xq = unpack_weight(x_words, x_scales)[:, unstriped(offs)]
    h = gelu(mxq(f64(w1), 0, "e4m3").T @ xq)
    low = 0.5 * (h[:, :V] + h[:, V:2 * V])
    high = 0.5 * (h[:, :V] - h[:, V:2 * V])
    return unpack_fp4(w2_words, w2_scales).T @ mxq(low, 0, "e4m3") + unpack_fp4(w3_words, w3_scales).T @ mxq(high, 0, "e4m3")

@@ -1,0 +1,159 @@
+from contextlib import ExitStack
+
+import concourse.mybir as mybir
+
+K, T, S, V, H, N = 512, 2048, 1024, 512, 512, 128
+FLOPS = 2 * K * H * S + 2 * 2 * H * N * V
+
+F32 = mybir.dt.float32
+BF16 = mybir.dt.bfloat16
+I32 = mybir.dt.int32
+U32 = mybir.dt.uint32
+U16 = mybir.dt.uint16
+U8 = mybir.dt.uint8
+FP8X4 = mybir.dt.float8_e4m3fn_x4
+FP4X4 = mybir.dt.float4_e2m1fn_x4
+GELU = mybir.ActivationFunctionType.Gelu_apprx_tanh
+COPY = mybir.ActivationFunctionType.Copy
+ADD = mybir.AluOpType.add
+SUBTRACT = mybir.AluOpType.subtract
+
+P = 128
+PACK = 4
+QUADRANTS = 4
+GROUP = 16
+CHUNK = 128
+CHUNKS = V // CHUNK
+GATHER = 256
+M_SCALAR = 88
+
+
+def load_scale_rows(queue, plane, rows):
+    for q in range(QUADRANTS):
+        queue.dma_start(
+            out=plane[32 * q : 32 * q + 4, :].bitcast(I32),
+            in_=rows[4 * q : 4 * q + 4, :].bitcast(I32),
+        )
+
+
+def tile_picked_haar_gelu_p_kernel(
+    tc, x_words, x_scales, w1, w2_words, w2_scales, w3_words, w3_scales, offs, out
+):
+    nc = tc.nc
+    with ExitStack() as ctx:
+        keep = ctx.enter_context(tc.tile_pool(name="keep", bufs=1))
+        h_psum = ctx.enter_context(tc.psum_pool(name="h_psum", bufs=6))
+        o_psum = ctx.enter_context(tc.psum_pool(name="o_psum", bufs=2))
+
+        offsets = keep.tile([P, S // GROUP], U16, name="offsets")
+        x_scale_table = keep.tile([P, T], U8, name="x_scale_table", align_bytes=64)
+        x_word_table = keep.tile([P, T], I32, name="x_word_table", align_bytes=64)
+        w1_raw = keep.tile([P, PACK, H], F32, name="w1_raw", align_bytes=64)
+        band_words = [keep.tile([P, 2 * N], U8, name="band_words%d" % b, align_bytes=64) for b in range(2)]
+        band_scales = [keep.tile([P, N], U8, name="band_scales%d" % b, align_bytes=64) for b in range(2)]
+
+        nc.vector.memset(x_scale_table[:].bitcast(I32), 0)
+        warm_in = keep.tile([P, 1], F32, name="warm_in")
+        warm_out = keep.tile([P, 1], F32, name="warm_out")
+        nc.gpsimd.memset(warm_in[:], 0.0)
+        nc.scalar.activation(out=warm_out[:], in_=warm_in[:], func=GELU)
+        for b in range(2):
+            nc.gpsimd.memset(band_scales[b][:].bitcast(I32), 0)
+
+        w1_rows = w1.rearrange("(p j) c -> p j c", j=PACK)
+        nc.sync.dma_start(offsets[:], offs)
+        nc.sync.dma_start(out=w1_raw[:, 0:2, :], in_=w1_rows[:, 0:2, :])
+        load_scale_rows(nc.sync, x_scale_table, x_scales[0])
+        nc.sync.dma_start(out=w1_raw[:, 2:4, :], in_=w1_rows[:, 2:4, :])
+        nc.sync.dma_start(out=x_word_table[:], in_=x_words[0].rearrange("p n r -> p (n r)").bitcast(I32))
+        for b, (words, scales) in enumerate(((w2_words, w2_scales), (w3_words, w3_scales))):
+            nc.sync.dma_start(out=band_words[b][:].bitcast(I32), in_=words[0].bitcast(I32))
+            load_scale_rows(nc.sync, band_scales[b], scales[0])
+
+        picked_scales = keep.tile([P, S], U8, name="picked_scales", align_bytes=64)
+        nc.vector.tensor_copy(picked_scales[:], x_scale_table[:].indirect(offsets[:]))
+
+        w1_bf16 = keep.tile([P, PACK * H], BF16, name="w1_bf16", align_bytes=64)
+        dealt = w1_bf16[:].rearrange("p (t m j) -> p m j t", t=PACK, j=PACK)
+        source = w1_raw[:].rearrange("p j (m t) -> p m j t", t=PACK)
+        nc.scalar.copy(out=dealt[:, :M_SCALAR], in_=source[:, :M_SCALAR])
+        nc.vector.tensor_copy(out=dealt[:, M_SCALAR:], in_=source[:, M_SCALAR:])
+        w1_codes = keep.tile([P, H], U32, name="w1_codes", align_bytes=64)
+        w1_scales = keep.tile([P, H], U8, name="w1_scales", align_bytes=64)
+        nc.vector.quantize_mx(out=w1_codes[:].bitcast(FP8X4), scales=w1_scales[:], in_=w1_bf16[:])
+
+        picked_words = {}
+        for g in range(V // GATHER):
+            for d in range(2):
+                first = d * V + g * GATHER
+                picked = keep.tile([P, GATHER], U32, name="picked_words%d_%d" % (d, g), align_bytes=64)
+                nc.vector.tensor_copy(
+                    picked[:],
+                    x_word_table[:].bitcast(U32).indirect(offsets[:, first // GROUP : (first + GATHER) // GROUP]),
+                )
+                picked_words[d, g] = picked
+
+        hidden = {}
+        for c in range(CHUNKS):
+            for d in range(2):
+                g, at = divmod(c * CHUNK, GATHER)
+                first = d * V + c * CHUNK
+                bank = h_psum.tile([P, PACK, CHUNK], F32, name="h_bank")
+                for t in range(PACK):
+                    nc.tensor.matmul_mx(
+                        out=bank[:, t, :],
+                        lhsT=w1_codes[:, t * P : (t + 1) * P].bitcast(FP8X4),
+                        lhsT_scale=w1_scales[:, t * P : (t + 1) * P],
+                        rhs=picked_words[d, g][:, at : at + CHUNK].bitcast(FP8X4),
+                        rhs_scale=picked_scales[:, first : first + CHUNK],
+                        start=True,
+                        stop=True,
+                    )
+                h = keep.tile([P, CHUNK * PACK], F32, name="hidden%d_%d" % (d, c), align_bytes=64)
+                nc.scalar.activation(
+                    out=h[:].rearrange("p (n t) -> p n t", t=PACK),
+                    in_=bank[:].rearrange("p t n -> p n t"),
+                    func=GELU,
+                )
+                hidden[d, c] = h
+
+        bands = {}
+        codes = {}
+
+        def make_band(b, c):
+            band = keep.tile([P, CHUNK * PACK], BF16, name="band%d_%d" % (b, c), align_bytes=64)
+            nc.vector.tensor_tensor(band[:], hidden[0, c][:], hidden[1, c][:], (ADD, SUBTRACT)[b])
+            bands[b, c] = band
+
+        def quantise_band(b, c):
+            words = keep.tile([P, CHUNK], U32, name="band_codes%d_%d" % (b, c), align_bytes=64)
+            scales = keep.tile([P, CHUNK], U8, name="band_code_scales%d_%d" % (b, c), align_bytes=64)
+            nc.vector.quantize_mx(out=words[:].bitcast(FP8X4), scales=scales[:], in_=bands[b, c][:])
+            codes[b, c] = (words, scales)
+
+        def finish(c):
+            acc = o_psum.tile([P, CHUNK], F32, name="o_bank")
+            for b in range(2):
+                words, scales = codes[b, c]
+                nc.tensor.matmul_mx(
+                    out=acc[:],
+                    lhsT=band_words[b][:].bitcast(FP4X4),
+                    lhsT_scale=band_scales[b][:],
+                    rhs=words[:].bitcast(FP8X4),
+                    rhs_scale=scales[:],
+                    start=(b == 0),
+                    stop=(b == 1),
+                )
+            result = keep.tile([P, CHUNK], F32, name="result%d" % c)
+            nc.scalar.activation(out=result[:], in_=acc[:], func=COPY, scale=0.5)
+            nc.sync.dma_start(out=out[:, c * CHUNK : (c + 1) * CHUNK], in_=result[:])
+
+        for c in range(CHUNKS):
+            make_band(0, c)
+            if c > 0:
+                quantise_band(1, c - 1)
+                finish(c - 1)
+            make_band(1, c)
+            quantise_band(0, c)
+        quantise_band(1, CHUNKS - 1)
+        finish(CHUNKS - 1)

@@ -25,7 +25,7 @@ GROUP = 16
 CHUNK = 128
 CHUNKS = V // CHUNK
 GATHER = 256
-M_SCALAR = 88
+M_FIRST = 72
 
 
 def load_scale_rows(queue, plane, rows):
@@ -48,7 +48,10 @@ def tile_picked_haar_gelu_p_kernel(
         offsets = keep.tile([P, S // GROUP], U16, name="offsets")
         x_scale_table = keep.tile([P, T], U8, name="x_scale_table", align_bytes=64)
         x_word_table = keep.tile([P, T], I32, name="x_word_table", align_bytes=64)
-        w1_raw = keep.tile([P, PACK, H], F32, name="w1_raw", align_bytes=64)
+        m_ranges = ((0, M_FIRST), (M_FIRST, P))
+        w1_raw = [
+            keep.tile([P, PACK, (m1 - m0) * PACK], F32, name="w1_raw%d" % m0, align_bytes=64) for m0, m1 in m_ranges
+        ]
         band_words = [keep.tile([P, 2 * N], U8, name="band_words%d" % b, align_bytes=64) for b in range(2)]
         band_scales = [keep.tile([P, N], U8, name="band_scales%d" % b, align_bytes=64) for b in range(2)]
 
@@ -61,10 +64,10 @@ def tile_picked_haar_gelu_p_kernel(
             nc.gpsimd.memset(band_scales[b][:].bitcast(I32), 0)
 
         w1_rows = w1.rearrange("(p j) c -> p j c", j=PACK)
+        nc.sync.dma_start(out=w1_raw[0][:], in_=w1_rows[:, :, : M_FIRST * PACK])
         nc.sync.dma_start(offsets[:], offs)
-        nc.sync.dma_start(out=w1_raw[:, 0:2, :], in_=w1_rows[:, 0:2, :])
         load_scale_rows(nc.sync, x_scale_table, x_scales[0])
-        nc.sync.dma_start(out=w1_raw[:, 2:4, :], in_=w1_rows[:, 2:4, :])
+        nc.sync.dma_start(out=w1_raw[1][:], in_=w1_rows[:, :, M_FIRST * PACK :])
         nc.sync.dma_start(out=x_word_table[:], in_=x_words[0].rearrange("p n r -> p (n r)").bitcast(I32))
         for b, (words, scales) in enumerate(((w2_words, w2_scales), (w3_words, w3_scales))):
             nc.sync.dma_start(out=band_words[b][:].bitcast(I32), in_=words[0].bitcast(I32))
@@ -75,9 +78,8 @@ def tile_picked_haar_gelu_p_kernel(
 
         w1_bf16 = keep.tile([P, PACK * H], BF16, name="w1_bf16", align_bytes=64)
         dealt = w1_bf16[:].rearrange("p (t m j) -> p m j t", t=PACK, j=PACK)
-        source = w1_raw[:].rearrange("p j (m t) -> p m j t", t=PACK)
-        nc.scalar.copy(out=dealt[:, :M_SCALAR], in_=source[:, :M_SCALAR])
-        nc.vector.tensor_copy(out=dealt[:, M_SCALAR:], in_=source[:, M_SCALAR:])
+        for raw, (m0, m1) in zip(w1_raw, m_ranges):
+            nc.scalar.copy(out=dealt[:, m0:m1], in_=raw[:].rearrange("p j (m t) -> p m j t", t=PACK))
         w1_codes = keep.tile([P, H], U32, name="w1_codes", align_bytes=64)
         w1_scales = keep.tile([P, H], U8, name="w1_scales", align_bytes=64)
         nc.vector.quantize_mx(out=w1_codes[:].bitcast(FP8X4), scales=w1_scales[:], in_=w1_bf16[:])
@@ -110,11 +112,14 @@ def tile_picked_haar_gelu_p_kernel(
                         stop=True,
                     )
                 h = keep.tile([P, CHUNK * PACK], F32, name="hidden%d_%d" % (d, c), align_bytes=64)
-                nc.scalar.activation(
-                    out=h[:].rearrange("p (n t) -> p n t", t=PACK),
-                    in_=bank[:].rearrange("p t n -> p n t"),
-                    func=GELU,
-                )
+                parts = 2 if (d, c) == (1, 0) else 1
+                for part in range(parts):
+                    cols = slice(part * CHUNK // parts, (part + 1) * CHUNK // parts)
+                    nc.scalar.activation(
+                        out=h[:].rearrange("p (n t) -> p n t", t=PACK)[:, cols],
+                        in_=bank[:].rearrange("p t n -> p n t")[:, cols],
+                        func=GELU,
+                    )
                 hidden[d, c] = h
 
         bands = {}
@@ -124,6 +129,17 @@ def tile_picked_haar_gelu_p_kernel(
             band = keep.tile([P, CHUNK * PACK], BF16, name="band%d_%d" % (b, c), align_bytes=64)
             nc.vector.tensor_tensor(band[:], hidden[0, c][:], hidden[1, c][:], (ADD, SUBTRACT)[b])
             bands[b, c] = band
+
+        def make_first_bands():
+            width = CHUNK * PACK // 2
+            for b in range(2):
+                bands[b, 0] = keep.tile([P, CHUNK * PACK], BF16, name="band%d_0" % b, align_bytes=64)
+            for part in range(2):
+                cols = slice(part * width, (part + 1) * width)
+                for b in range(2):
+                    nc.vector.tensor_tensor(
+                        bands[b, 0][:, cols], hidden[0, 0][:, cols], hidden[1, 0][:, cols], (ADD, SUBTRACT)[b]
+                    )
 
         def quantise_band(b, c):
             words = keep.tile([P, CHUNK], U32, name="band_codes%d_%d" % (b, c), align_bytes=64)
@@ -148,11 +164,12 @@ def tile_picked_haar_gelu_p_kernel(
             nc.scalar.activation(out=result[:], in_=acc[:], func=COPY, scale=0.5)
             nc.sync.dma_start(out=out[:, c * CHUNK : (c + 1) * CHUNK], in_=result[:])
 
-        for c in range(CHUNKS):
+        make_first_bands()
+        quantise_band(0, 0)
+        for c in range(1, CHUNKS):
             make_band(0, c)
-            if c > 0:
-                quantise_band(1, c - 1)
-                finish(c - 1)
+            quantise_band(1, c - 1)
+            finish(c - 1)
             make_band(1, c)
             quantise_band(0, c)
         quantise_band(1, CHUNKS - 1)

@@ -56,10 +56,6 @@ def tile_picked_haar_gelu_p_kernel(
         band_scales = [keep.tile([P, N], U8, name="band_scales%d" % b, align_bytes=64) for b in range(2)]
 
         nc.vector.memset(x_scale_table[:].bitcast(I32), 0)
-        warm_in = keep.tile([P, 1], F32, name="warm_in")
-        warm_out = keep.tile([P, 1], F32, name="warm_out")
-        nc.gpsimd.memset(warm_in[:], 0.0)
-        nc.scalar.activation(out=warm_out[:], in_=warm_in[:], func=GELU)
         for b in range(2):
             nc.gpsimd.memset(band_scales[b][:].bitcast(I32), 0)
 

@@ -20,7 +20,6 @@ SUBTRACT = mybir.AluOpType.subtract
 
 P = 128
 PACK = 4
-QUADRANTS = 4
 GROUP = 16
 CHUNK = 128
 CHUNKS = V // CHUNK
@@ -29,10 +28,10 @@ M_FIRST = 72
 
 
 def load_scale_rows(queue, plane, rows):
-    for q in range(QUADRANTS):
+    for r in range(4):
         queue.dma_start(
-            out=plane[32 * q : 32 * q + 4, :].bitcast(I32),
-            in_=rows[4 * q : 4 * q + 4, :].bitcast(I32),
+            out=plane[r:P:32, :].bitcast(I32),
+            in_=rows[r:16:4, :].bitcast(I32),
         )
 
 

@@ -1,6 +1,7 @@
 from contextlib import ExitStack
 
 import concourse.mybir as mybir
+from concourse.masks import make_identity
 
 K, T, S, V, H, N = 512, 2048, 1024, 512, 512, 128
 FLOPS = 2 * K * H * S + 2 * 2 * H * N * V
@@ -25,6 +26,7 @@ CHUNK = 128
 CHUNKS = V // CHUNK
 GATHER = 256
 M_FIRST = 72
+TURNED = 2
 
 
 def load_scale_rows(queue, plane, rows):
@@ -53,10 +55,12 @@ def tile_picked_haar_gelu_p_kernel(
         ]
         band_words = [keep.tile([P, 2 * N], U8, name="band_words%d" % b, align_bytes=64) for b in range(2)]
         band_scales = [keep.tile([P, N], U8, name="band_scales%d" % b, align_bytes=64) for b in range(2)]
+        identity = keep.tile([P, P], F32, name="identity", align_bytes=64)
 
         nc.vector.memset(x_scale_table[:].bitcast(I32), 0)
         for b in range(2):
             nc.gpsimd.memset(band_scales[b][:].bitcast(I32), 0)
+        make_identity(nc, identity[:])
 
         w1_rows = w1.rearrange("(p j) c -> p j c", j=PACK)
         nc.sync.dma_start(out=w1_raw[0][:], in_=w1_rows[:, :, : M_FIRST * PACK])
@@ -95,18 +99,34 @@ def tile_picked_haar_gelu_p_kernel(
             for d in range(2):
                 g, at = divmod(c * CHUNK, GATHER)
                 first = d * V + c * CHUNK
+                tokens = picked_words[d, g][:, at : at + CHUNK].bitcast(FP8X4)
+                token_scales = picked_scales[:, first : first + CHUNK]
                 bank = h_psum.tile([P, PACK, CHUNK], F32, name="h_bank")
+                h = keep.tile([P, CHUNK * PACK], F32, name="hidden%d_%d" % (d, c), align_bytes=64)
+                hidden[d, c] = h
+                if c == TURNED:
+                    flat = bank[:].rearrange("p t n -> p (t n)")
+                    nc.tensor.matmul_mx(
+                        out=flat,
+                        lhsT=tokens,
+                        lhsT_scale=token_scales,
+                        rhs=w1_codes[:].bitcast(FP8X4),
+                        rhs_scale=w1_scales[:],
+                        start=True,
+                        stop=True,
+                    )
+                    nc.scalar.activation(out=h[:], in_=flat, func=GELU)
+                    continue
                 for t in range(PACK):
                     nc.tensor.matmul_mx(
                         out=bank[:, t, :],
                         lhsT=w1_codes[:, t * P : (t + 1) * P].bitcast(FP8X4),
                         lhsT_scale=w1_scales[:, t * P : (t + 1) * P],
-                        rhs=picked_words[d, g][:, at : at + CHUNK].bitcast(FP8X4),
-                        rhs_scale=picked_scales[:, first : first + CHUNK],
+                        rhs=tokens,
+                        rhs_scale=token_scales,
                         start=True,
                         stop=True,
                     )
-                h = keep.tile([P, CHUNK * PACK], F32, name="hidden%d_%d" % (d, c), align_bytes=64)
                 parts = 2 if (d, c) == (1, 0) else 1
                 for part in range(parts):
                     cols = slice(part * CHUNK // parts, (part + 1) * CHUNK // parts)
@@ -115,7 +135,6 @@ def tile_picked_haar_gelu_p_kernel(
                         in_=bank[:].rearrange("p t n -> p n t")[:, cols],
                         func=GELU,
                     )
-                hidden[d, c] = h
 
         bands = {}
         codes = {}
@@ -135,6 +154,24 @@ def tile_picked_haar_gelu_p_kernel(
                     nc.vector.tensor_tensor(
                         bands[b, 0][:, cols], hidden[0, 0][:, cols], hidden[1, 0][:, cols], (ADD, SUBTRACT)[b]
                     )
+
+        def turn_band(b, second):
+            bank = h_psum.tile([P, PACK, CHUNK], F32, name="h_bank")
+            for t in range(PACK):
+                for member, last in ((hidden[0, TURNED], False), (second, True)):
+                    nc.tensor.matmul(
+                        out=bank[:, t, :],
+                        lhsT=member[:, t * P : (t + 1) * P],
+                        rhs=identity[:],
+                        is_transpose=True,
+                        start=not last,
+                        stop=last,
+                    )
+            band = keep.tile([P, CHUNK * PACK], BF16, name="band%d_%d" % (b, TURNED), align_bytes=64)
+            nc.scalar.copy(
+                out=band[:].rearrange("p (n t) -> p n t", t=PACK), in_=bank[:].rearrange("p t n -> p n t")
+            )
+            bands[b, TURNED] = band
 
         def quantise_band(b, c):
             words = keep.tile([P, CHUNK], U32, name="band_codes%d_%d" % (b, c), align_bytes=64)
@@ -161,11 +198,22 @@ def tile_picked_haar_gelu_p_kernel(
 
         make_first_bands()
         quantise_band(0, 0)
-        for c in range(1, CHUNKS):
-            make_band(0, c)
-            quantise_band(1, c - 1)
-            finish(c - 1)
-            make_band(1, c)
-            quantise_band(0, c)
-        quantise_band(1, CHUNKS - 1)
-        finish(CHUNKS - 1)
+        make_band(0, 1)
+        quantise_band(1, 0)
+        make_band(1, 1)
+        quantise_band(0, 1)
+        negated = keep.tile([P, CHUNK * PACK], F32, name="negated", align_bytes=64)
+        nc.vector.tensor_scalar_mul(negated[:], hidden[1, TURNED][:], -1.0)
+        quantise_band(1, 1)
+        turn_band(0, hidden[1, TURNED])
+        turn_band(1, negated)
+        finish(0)
+        finish(1)
+        make_band(0, 3)
+        make_band(1, 3)
+        quantise_band(0, TURNED)
+        quantise_band(1, TURNED)
+        finish(TURNED)
+        quantise_band(0, 3)
+        quantise_band(1, 3)
+        finish(3)

@@ -43,7 +43,8 @@ def tile_picked_haar_gelu_p_kernel(
     nc = tc.nc
     with ExitStack() as ctx:
         keep = ctx.enter_context(tc.tile_pool(name="keep", bufs=1))
-        h_psum = ctx.enter_context(tc.psum_pool(name="h_psum", bufs=6))
+        h_psum = ctx.enter_context(tc.psum_pool(name="h_psum", bufs=3))
+        t_psum = ctx.enter_context(tc.psum_pool(name="t_psum", bufs=2))
         o_psum = ctx.enter_context(tc.psum_pool(name="o_psum", bufs=2))
 
         offsets = keep.tile([P, S // GROUP], U16, name="offsets")
@@ -156,16 +157,16 @@ def tile_picked_haar_gelu_p_kernel(
                     )
 
         def turn_band(b, second):
-            bank = h_psum.tile([P, PACK, CHUNK], F32, name="h_bank")
-            for t in range(PACK):
-                for member, last in ((hidden[0, TURNED], False), (second, True)):
+            bank = t_psum.tile([P, PACK, CHUNK], F32, name="t_bank")
+            for d, member in enumerate((hidden[0, TURNED], second)):
+                for t in range(PACK):
                     nc.tensor.matmul(
                         out=bank[:, t, :],
                         lhsT=member[:, t * P : (t + 1) * P],
                         rhs=identity[:],
                         is_transpose=True,
-                        start=not last,
-                        stop=last,
+                        start=(d, t) == (0, 0),
+                        stop=(d, t) == (1, PACK - 1),
                     )
             band = keep.tile([P, CHUNK * PACK], BF16, name="band%d_%d" % (b, TURNED), align_bytes=64)
             nc.scalar.copy(

@@ -25,7 +25,8 @@ GROUP = 16
 CHUNK = 128
 CHUNKS = V // CHUNK
 GATHER = 256
-M_FIRST = 72
+M_SCALAR = 72
+M_EARLY = 8
 TURNED = 2
 
 
@@ -50,24 +51,21 @@ def tile_picked_haar_gelu_p_kernel(
         offsets = keep.tile([P, S // GROUP], U16, name="offsets")
         x_scale_table = keep.tile([P, T], U8, name="x_scale_table", align_bytes=64)
         x_word_table = keep.tile([P, T], I32, name="x_word_table", align_bytes=64)
-        m_ranges = ((0, M_FIRST), (M_FIRST, P))
-        w1_raw = [
-            keep.tile([P, PACK, (m1 - m0) * PACK], F32, name="w1_raw%d" % m0, align_bytes=64) for m0, m1 in m_ranges
-        ]
+        w1_raw = keep.tile([P, PACK, H], F32, name="w1_raw", align_bytes=64)
         band_words = [keep.tile([P, 2 * N], U8, name="band_words%d" % b, align_bytes=64) for b in range(2)]
         band_scales = [keep.tile([P, N], U8, name="band_scales%d" % b, align_bytes=64) for b in range(2)]
         identity = keep.tile([P, P], F32, name="identity", align_bytes=64)
 
-        nc.vector.memset(x_scale_table[:].bitcast(I32), 0)
+        nc.gpsimd.memset(x_scale_table[:].bitcast(I32), 0)
         for b in range(2):
-            nc.gpsimd.memset(band_scales[b][:].bitcast(I32), 0)
+            nc.vector.memset(band_scales[b][:].bitcast(I32), 0)
         make_identity(nc, identity[:])
 
         w1_rows = w1.rearrange("(p j) c -> p j c", j=PACK)
-        nc.sync.dma_start(out=w1_raw[0][:], in_=w1_rows[:, :, : M_FIRST * PACK])
+        nc.sync.dma_start(out=w1_raw[:, :1, :], in_=w1_rows[:, :1, :])
         nc.sync.dma_start(offsets[:], offs)
         load_scale_rows(nc.sync, x_scale_table, x_scales[0])
-        nc.sync.dma_start(out=w1_raw[1][:], in_=w1_rows[:, :, M_FIRST * PACK :])
+        nc.sync.dma_start(out=w1_raw[:, 1:, :], in_=w1_rows[:, 1:, :])
         nc.sync.dma_start(out=x_word_table[:], in_=x_words[0].rearrange("p n r -> p (n r)").bitcast(I32))
         for b, (words, scales) in enumerate(((w2_words, w2_scales), (w3_words, w3_scales))):
             nc.sync.dma_start(out=band_words[b][:].bitcast(I32), in_=words[0].bitcast(I32))
@@ -78,8 +76,11 @@ def tile_picked_haar_gelu_p_kernel(
 
         w1_bf16 = keep.tile([P, PACK * H], BF16, name="w1_bf16", align_bytes=64)
         dealt = w1_bf16[:].rearrange("p (t m j) -> p m j t", t=PACK, j=PACK)
-        for raw, (m0, m1) in zip(w1_raw, m_ranges):
-            nc.scalar.copy(out=dealt[:, m0:m1], in_=raw[:].rearrange("p j (m t) -> p m j t", t=PACK))
+        undealt = w1_raw[:].rearrange("p j (m t) -> p m j t", t=PACK)
+        nc.scalar.copy(out=dealt[:, :M_EARLY, :1], in_=undealt[:, :M_EARLY, :1])
+        nc.scalar.copy(out=dealt[:, :M_EARLY, 1:], in_=undealt[:, :M_EARLY, 1:])
+        nc.scalar.copy(out=dealt[:, M_EARLY:M_SCALAR], in_=undealt[:, M_EARLY:M_SCALAR])
+        nc.vector.tensor_copy(out=dealt[:, M_SCALAR:], in_=undealt[:, M_SCALAR:])
         w1_codes = keep.tile([P, H], U32, name="w1_codes", align_bytes=64)
         w1_scales = keep.tile([P, H], U8, name="w1_scales", align_bytes=64)
         nc.vector.quantize_mx(out=w1_codes[:].bitcast(FP8X4), scales=w1_scales[:], in_=w1_bf16[:])

@@ -25,9 +25,10 @@ GROUP = 16
 CHUNK = 128
 CHUNKS = V // CHUNK
 GATHER = 256
-M_SCALAR = 72
+T_SCALAR = 2
 M_EARLY = 8
 TURNED = 2
+LAST = TURNED
 
 
 def load_scale_rows(queue, plane, rows):
@@ -77,13 +78,16 @@ def tile_picked_haar_gelu_p_kernel(
         w1_bf16 = keep.tile([P, PACK * H], BF16, name="w1_bf16", align_bytes=64)
         dealt = w1_bf16[:].rearrange("p (t m j) -> p m j t", t=PACK, j=PACK)
         undealt = w1_raw[:].rearrange("p j (m t) -> p m j t", t=PACK)
-        nc.scalar.copy(out=dealt[:, :M_EARLY, :1], in_=undealt[:, :M_EARLY, :1])
-        nc.scalar.copy(out=dealt[:, :M_EARLY, 1:], in_=undealt[:, :M_EARLY, 1:])
-        nc.scalar.copy(out=dealt[:, M_EARLY:M_SCALAR], in_=undealt[:, M_EARLY:M_SCALAR])
-        nc.vector.tensor_copy(out=dealt[:, M_SCALAR:], in_=undealt[:, M_SCALAR:])
+        nc.scalar.copy(out=dealt[:, :M_EARLY, :1, :T_SCALAR], in_=undealt[:, :M_EARLY, :1, :T_SCALAR])
+        nc.scalar.copy(out=dealt[:, :M_EARLY, 1:, :T_SCALAR], in_=undealt[:, :M_EARLY, 1:, :T_SCALAR])
+        nc.scalar.copy(out=dealt[:, M_EARLY:, :, :T_SCALAR], in_=undealt[:, M_EARLY:, :, :T_SCALAR])
+        nc.vector.tensor_copy(out=dealt[:, :, :, T_SCALAR:], in_=undealt[:, :, :, T_SCALAR:])
         w1_codes = keep.tile([P, H], U32, name="w1_codes", align_bytes=64)
         w1_scales = keep.tile([P, H], U8, name="w1_scales", align_bytes=64)
-        nc.vector.quantize_mx(out=w1_codes[:].bitcast(FP8X4), scales=w1_scales[:], in_=w1_bf16[:])
+        for c0, c1 in ((0, T_SCALAR * P), (T_SCALAR * P, H)):
+            nc.vector.quantize_mx(
+                out=w1_codes[:, c0:c1].bitcast(FP8X4), scales=w1_scales[:, c0:c1], in_=w1_bf16[:, PACK * c0 : PACK * c1]
+            )
 
         picked_words = {}
         for g in range(V // GATHER):
@@ -129,7 +133,7 @@ def tile_picked_haar_gelu_p_kernel(
                         start=True,
                         stop=True,
                     )
-                parts = 2 if (d, c) == (1, 0) else 1
+                parts = 2 if d == 1 and c in (0, CHUNKS - 1) else 1
                 for part in range(parts):
                     cols = slice(part * CHUNK // parts, (part + 1) * CHUNK // parts)
                     nc.scalar.activation(
@@ -146,15 +150,15 @@ def tile_picked_haar_gelu_p_kernel(
             nc.vector.tensor_tensor(band[:], hidden[0, c][:], hidden[1, c][:], (ADD, SUBTRACT)[b])
             bands[b, c] = band
 
-        def make_first_bands():
+        def make_bands_by_halves(c):
             width = CHUNK * PACK // 2
             for b in range(2):
-                bands[b, 0] = keep.tile([P, CHUNK * PACK], BF16, name="band%d_0" % b, align_bytes=64)
+                bands[b, c] = keep.tile([P, CHUNK * PACK], BF16, name="band%d_%d" % (b, c), align_bytes=64)
             for part in range(2):
                 cols = slice(part * width, (part + 1) * width)
                 for b in range(2):
                     nc.vector.tensor_tensor(
-                        bands[b, 0][:, cols], hidden[0, 0][:, cols], hidden[1, 0][:, cols], (ADD, SUBTRACT)[b]
+                        bands[b, c][:, cols], hidden[0, c][:, cols], hidden[1, c][:, cols], (ADD, SUBTRACT)[b]
                     )
 
         def turn_band(b, second):
@@ -195,10 +199,13 @@ def tile_picked_haar_gelu_p_kernel(
                     stop=(b == 1),
                 )
             result = keep.tile([P, CHUNK], F32, name="result%d" % c)
-            nc.scalar.activation(out=result[:], in_=acc[:], func=COPY, scale=0.5)
+            if c == LAST:
+                nc.vector.tensor_scalar_mul(result[:], acc[:], 0.5)
+            else:
+                nc.scalar.activation(out=result[:], in_=acc[:], func=COPY, scale=0.5)
             nc.sync.dma_start(out=out[:, c * CHUNK : (c + 1) * CHUNK], in_=result[:])
 
-        make_first_bands()
+        make_bands_by_halves(0)
         quantise_band(0, 0)
         make_band(0, 1)
         quantise_band(1, 0)
@@ -211,11 +218,10 @@ def tile_picked_haar_gelu_p_kernel(
         turn_band(1, negated)
         finish(0)
         finish(1)
-        make_band(0, 3)
-        make_band(1, 3)
+        make_bands_by_halves(3)
         quantise_band(0, TURNED)
-        quantise_band(1, TURNED)
-        finish(TURNED)
         quantise_band(0, 3)
         quantise_band(1, 3)
         finish(3)
+        quantise_band(1, TURNED)
+        finish(TURNED)

@@ -27,6 +27,7 @@ CHUNKS = V // CHUNK
 GATHER = 256
 T_SCALAR = 2
 M_EARLY = 8
+M_SHARED = 32
 TURNED = 2
 LAST = TURNED
 
@@ -45,49 +46,61 @@ def tile_picked_haar_gelu_p_kernel(
     nc = tc.nc
     with ExitStack() as ctx:
         keep = ctx.enter_context(tc.tile_pool(name="keep", bufs=1))
+        early = ctx.enter_context(tc.tile_pool(name="early", bufs=1))
         h_psum = ctx.enter_context(tc.psum_pool(name="h_psum", bufs=3))
         t_psum = ctx.enter_context(tc.psum_pool(name="t_psum", bufs=2))
         o_psum = ctx.enter_context(tc.psum_pool(name="o_psum", bufs=2))
 
         offsets = keep.tile([P, S // GROUP], U16, name="offsets")
         x_scale_table = keep.tile([P, T], U8, name="x_scale_table", align_bytes=64)
+        pieces = ((0, S - GATHER), (S - GATHER, S))
+        picked_scales = [keep.tile([P, e1 - e0], U8, name="picked_scales%d" % e0, align_bytes=64) for e0, e1 in pieces]
         x_word_table = keep.tile([P, T], I32, name="x_word_table", align_bytes=64)
         w1_raw = keep.tile([P, PACK, H], F32, name="w1_raw", align_bytes=64)
-        band_words = [keep.tile([P, 2 * N], U8, name="band_words%d" % b, align_bytes=64) for b in range(2)]
-        band_scales = [keep.tile([P, N], U8, name="band_scales%d" % b, align_bytes=64) for b in range(2)]
         identity = keep.tile([P, P], F32, name="identity", align_bytes=64)
 
         nc.gpsimd.memset(x_scale_table[:].bitcast(I32), 0)
-        for b in range(2):
-            nc.vector.memset(band_scales[b][:].bitcast(I32), 0)
+        for plane in picked_scales:
+            nc.vector.memset(plane[:].bitcast(I32), 0)
         make_identity(nc, identity[:])
 
         w1_rows = w1.rearrange("(p j) c -> p j c", j=PACK)
         nc.sync.dma_start(out=w1_raw[:, :1, :], in_=w1_rows[:, :1, :])
         nc.sync.dma_start(offsets[:], offs)
-        load_scale_rows(nc.sync, x_scale_table, x_scales[0])
+        nc.sync.dma_start(out=x_scale_table[0:P:8, :].bitcast(I32), in_=x_scales[0].bitcast(I32))
         nc.sync.dma_start(out=w1_raw[:, 1:, :], in_=w1_rows[:, 1:, :])
         nc.sync.dma_start(out=x_word_table[:], in_=x_words[0].rearrange("p n r -> p (n r)").bitcast(I32))
-        for b, (words, scales) in enumerate(((w2_words, w2_scales), (w3_words, w3_scales))):
-            nc.sync.dma_start(out=band_words[b][:].bitcast(I32), in_=words[0].bitcast(I32))
-            load_scale_rows(nc.sync, band_scales[b], scales[0])
 
-        picked_scales = keep.tile([P, S], U8, name="picked_scales", align_bytes=64)
-        nc.vector.tensor_copy(picked_scales[:], x_scale_table[:].indirect(offsets[:]))
+        for plane, (e0, e1) in zip(picked_scales, pieces):
+            spread = keep.tile([P, e1 - e0], U8, name="spread_scales%d" % e0, align_bytes=64)
+            nc.vector.tensor_copy(spread[:], x_scale_table[:].indirect(offsets[:, e0 // GROUP : e1 // GROUP]))
+            for r in range(4):
+                nc.sync.dma_start(out=plane[r:P:32, :].bitcast(I32), in_=spread[8 * r : P : 32, :].bitcast(I32))
 
-        w1_bf16 = keep.tile([P, PACK * H], BF16, name="w1_bf16", align_bytes=64)
+        w1_bf16 = early.tile([P, PACK * H], BF16, name="w1_bf16", align_bytes=64, offset=0)
         dealt = w1_bf16[:].rearrange("p (t m j) -> p m j t", t=PACK, j=PACK)
         undealt = w1_raw[:].rearrange("p j (m t) -> p m j t", t=PACK)
         nc.scalar.copy(out=dealt[:, :M_EARLY, :1, :T_SCALAR], in_=undealt[:, :M_EARLY, :1, :T_SCALAR])
         nc.scalar.copy(out=dealt[:, :M_EARLY, 1:, :T_SCALAR], in_=undealt[:, :M_EARLY, 1:, :T_SCALAR])
         nc.scalar.copy(out=dealt[:, M_EARLY:, :, :T_SCALAR], in_=undealt[:, M_EARLY:, :, :T_SCALAR])
-        nc.vector.tensor_copy(out=dealt[:, :, :, T_SCALAR:], in_=undealt[:, :, :, T_SCALAR:])
+        nc.scalar.copy(out=dealt[:, :M_SHARED, :, T_SCALAR:], in_=undealt[:, :M_SHARED, :, T_SCALAR:])
+        nc.vector.tensor_copy(out=dealt[:, M_SHARED:, :, T_SCALAR:], in_=undealt[:, M_SHARED:, :, T_SCALAR:])
         w1_codes = keep.tile([P, H], U32, name="w1_codes", align_bytes=64)
         w1_scales = keep.tile([P, H], U8, name="w1_scales", align_bytes=64)
         for c0, c1 in ((0, T_SCALAR * P), (T_SCALAR * P, H)):
             nc.vector.quantize_mx(
                 out=w1_codes[:, c0:c1].bitcast(FP8X4), scales=w1_scales[:, c0:c1], in_=w1_bf16[:, PACK * c0 : PACK * c1]
             )
+
+        band_words = []
+        band_scales = []
+        for b, (words, scales) in enumerate(((w2_words, w2_scales), (w3_words, w3_scales))):
+            at = b * 3 * N
+            band_words.append(early.tile([P, 2 * N], U8, name="band_words%d" % b, align_bytes=64, offset=at))
+            band_scales.append(early.tile([P, N], U8, name="band_scales%d" % b, align_bytes=64, offset=at + 2 * N))
+            nc.gpsimd.memset(band_scales[b][:].bitcast(I32), 0)
+            nc.sync.dma_start(out=band_words[b][:].bitcast(I32), in_=words[0].bitcast(I32))
+            load_scale_rows(nc.sync, band_scales[b], scales[0])
 
         picked_words = {}
         for g in range(V // GATHER):
@@ -106,7 +119,8 @@ def tile_picked_haar_gelu_p_kernel(
                 g, at = divmod(c * CHUNK, GATHER)
                 first = d * V + c * CHUNK
                 tokens = picked_words[d, g][:, at : at + CHUNK].bitcast(FP8X4)
-                token_scales = picked_scales[:, first : first + CHUNK]
+                late = (d, g) == (1, 1)
+                token_scales = picked_scales[1][:, at : at + CHUNK] if late else picked_scales[0][:, first : first + CHUNK]
                 bank = h_psum.tile([P, PACK, CHUNK], F32, name="h_bank")
                 h = keep.tile([P, CHUNK * PACK], F32, name="hidden%d_%d" % (d, c), align_bytes=64)
                 hidden[d, c] = h

@@ -30,6 +30,7 @@ M_EARLY = 8
 M_SHARED = 32
 TURNED = 2
 LAST = TURNED
+WARM_UPS = 4
 
 
 def load_scale_rows(queue, plane, rows):
@@ -49,6 +50,7 @@ def tile_picked_haar_gelu_p_kernel(
         early = ctx.enter_context(tc.tile_pool(name="early", bufs=1))
         h_psum = ctx.enter_context(tc.psum_pool(name="h_psum", bufs=3))
         t_psum = ctx.enter_context(tc.psum_pool(name="t_psum", bufs=2))
+        w_psum = ctx.enter_context(tc.psum_pool(name="w_psum", bufs=1))
         o_psum = ctx.enter_context(tc.psum_pool(name="o_psum", bufs=2))
 
         offsets = keep.tile([P, S // GROUP], U16, name="offsets")
@@ -90,6 +92,18 @@ def tile_picked_haar_gelu_p_kernel(
         for c0, c1 in ((0, T_SCALAR * P), (T_SCALAR * P, H)):
             nc.vector.quantize_mx(
                 out=w1_codes[:, c0:c1].bitcast(FP8X4), scales=w1_scales[:, c0:c1], in_=w1_bf16[:, PACK * c0 : PACK * c1]
+            )
+
+        warm = w_psum.tile([P, 2 * P], F32, name="warm")
+        for rep in range(WARM_UPS):
+            nc.tensor.matmul_mx(
+                out=warm[:],
+                lhsT=w1_codes[:, :P].bitcast(FP8X4),
+                lhsT_scale=w1_scales[:, :P],
+                rhs=w1_codes[:, : 2 * P].bitcast(FP8X4),
+                rhs_scale=w1_scales[:, : 2 * P],
+                start=True,
+                stop=True,
             )
 
         band_words = []

@@ -24,13 +24,16 @@ PACK = 4
 GROUP = 16
 CHUNK = 128
 CHUNKS = V // CHUNK
-GATHER = 256
+GATHERS = ((0, 128), (512, 768), (128, 384), (768, 1024), (384, 512))
+LATE = 256
+ROW_FIRST, ROW_STEP = 11, 7
+LEAD = 512
 T_SCALAR = 2
 M_EARLY = 8
 M_SHARED = 32
 TURNED = 2
 LAST = TURNED
-WARM_UPS = 4
+WARM_UPS = 2
 
 
 def load_scale_rows(queue, plane, rows):
@@ -55,10 +58,10 @@ def tile_picked_haar_gelu_p_kernel(
 
         offsets = keep.tile([P, S // GROUP], U16, name="offsets")
         x_scale_table = keep.tile([P, T], U8, name="x_scale_table", align_bytes=64)
-        pieces = ((0, S - GATHER), (S - GATHER, S))
+        pieces = ((0, S - LATE), (S - LATE, S))
         picked_scales = [keep.tile([P, e1 - e0], U8, name="picked_scales%d" % e0, align_bytes=64) for e0, e1 in pieces]
         x_word_table = keep.tile([P, T], I32, name="x_word_table", align_bytes=64)
-        w1_raw = keep.tile([P, PACK, H], F32, name="w1_raw", align_bytes=64)
+        w1_raw = keep.tile([P, PACK * H], F32, name="w1_raw", align_bytes=64)
         identity = keep.tile([P, P], F32, name="identity", align_bytes=64)
 
         nc.gpsimd.memset(x_scale_table[:].bitcast(I32), 0)
@@ -66,22 +69,26 @@ def tile_picked_haar_gelu_p_kernel(
             nc.vector.memset(plane[:].bitcast(I32), 0)
         make_identity(nc, identity[:])
 
-        w1_rows = w1.rearrange("(p j) c -> p j c", j=PACK)
-        nc.sync.dma_start(out=w1_raw[:, :1, :], in_=w1_rows[:, :1, :])
+        w1_rows = w1.rearrange("(p j) c -> p (j c)", j=PACK)
+        nc.sync.dma_start(out=w1_raw[:, :LEAD], in_=w1_rows[:, :LEAD])
         nc.sync.dma_start(offsets[:], offs)
-        nc.sync.dma_start(out=x_scale_table[0:P:8, :].bitcast(I32), in_=x_scales[0].bitcast(I32))
-        nc.sync.dma_start(out=w1_raw[:, 1:, :], in_=w1_rows[:, 1:, :])
+        nc.sync.dma_start(out=x_scale_table[ROW_FIRST : ROW_FIRST + 16 * ROW_STEP : ROW_STEP, :].bitcast(I32), in_=x_scales[0].bitcast(I32))
+        nc.sync.dma_start(out=w1_raw[:, LEAD:], in_=w1_rows[:, LEAD:])
         nc.sync.dma_start(out=x_word_table[:], in_=x_words[0].rearrange("p n r -> p (n r)").bitcast(I32))
 
         for plane, (e0, e1) in zip(picked_scales, pieces):
             spread = keep.tile([P, e1 - e0], U8, name="spread_scales%d" % e0, align_bytes=64)
             nc.vector.tensor_copy(spread[:], x_scale_table[:].indirect(offsets[:, e0 // GROUP : e1 // GROUP]))
             for r in range(4):
-                nc.sync.dma_start(out=plane[r:P:32, :].bitcast(I32), in_=spread[8 * r : P : 32, :].bitcast(I32))
+                row = ROW_FIRST + r * ROW_STEP
+                nc.sync.dma_start(
+                    out=plane[r:P:32, :].bitcast(I32),
+                    in_=spread[row : row + 12 * ROW_STEP + 1 : 4 * ROW_STEP, :].bitcast(I32),
+                )
 
         w1_bf16 = early.tile([P, PACK * H], BF16, name="w1_bf16", align_bytes=64, offset=0)
         dealt = w1_bf16[:].rearrange("p (t m j) -> p m j t", t=PACK, j=PACK)
-        undealt = w1_raw[:].rearrange("p j (m t) -> p m j t", t=PACK)
+        undealt = w1_raw[:].rearrange("p (j m t) -> p m j t", j=PACK, t=PACK)
         nc.scalar.copy(out=dealt[:, :M_EARLY, :1, :T_SCALAR], in_=undealt[:, :M_EARLY, :1, :T_SCALAR])
         nc.scalar.copy(out=dealt[:, :M_EARLY, 1:, :T_SCALAR], in_=undealt[:, :M_EARLY, 1:, :T_SCALAR])
         nc.scalar.copy(out=dealt[:, M_EARLY:, :, :T_SCALAR], in_=undealt[:, M_EARLY:, :, :T_SCALAR])
@@ -117,24 +124,21 @@ def tile_picked_haar_gelu_p_kernel(
             load_scale_rows(nc.sync, band_scales[b], scales[0])
 
         picked_words = {}
-        for g in range(V // GATHER):
-            for d in range(2):
-                first = d * V + g * GATHER
-                picked = keep.tile([P, GATHER], U32, name="picked_words%d_%d" % (d, g), align_bytes=64)
-                nc.vector.tensor_copy(
-                    picked[:],
-                    x_word_table[:].bitcast(U32).indirect(offsets[:, first // GROUP : (first + GATHER) // GROUP]),
-                )
-                picked_words[d, g] = picked
+        for e0, e1 in GATHERS:
+            picked = keep.tile([P, e1 - e0], U32, name="picked_words%d" % e0, align_bytes=64)
+            nc.vector.tensor_copy(
+                picked[:], x_word_table[:].bitcast(U32).indirect(offsets[:, e0 // GROUP : e1 // GROUP])
+            )
+            for first in range(e0, e1, CHUNK):
+                picked_words[first] = picked[:, first - e0 : first - e0 + CHUNK]
 
         hidden = {}
         for c in range(CHUNKS):
             for d in range(2):
-                g, at = divmod(c * CHUNK, GATHER)
                 first = d * V + c * CHUNK
-                tokens = picked_words[d, g][:, at : at + CHUNK].bitcast(FP8X4)
-                late = (d, g) == (1, 1)
-                token_scales = picked_scales[1][:, at : at + CHUNK] if late else picked_scales[0][:, first : first + CHUNK]
+                tokens = picked_words[first].bitcast(FP8X4)
+                piece, at = divmod(first, S - LATE)
+                token_scales = picked_scales[piece][:, at : at + CHUNK]
                 bank = h_psum.tile([P, PACK, CHUNK], F32, name="h_bank")
                 h = keep.tile([P, CHUNK * PACK], F32, name="hidden%d_%d" % (d, c), align_bytes=64)
                 hidden[d, c] = h

@@ -36,11 +36,12 @@ LAST = TURNED
 WARM_UPS = 2
 
 
-def load_scale_rows(queue, plane, rows):
+def move_scale_rows(nc, plane, spread):
     for r in range(4):
-        queue.dma_start(
+        row = ROW_FIRST + r * ROW_STEP
+        nc.sync.dma_start(
             out=plane[r:P:32, :].bitcast(I32),
-            in_=rows[r:16:4, :].bitcast(I32),
+            in_=spread[row : row + 12 * ROW_STEP + 1 : 4 * ROW_STEP, :].bitcast(I32),
         )
 
 
@@ -53,8 +54,7 @@ def tile_picked_haar_gelu_p_kernel(
         early = ctx.enter_context(tc.tile_pool(name="early", bufs=1))
         h_psum = ctx.enter_context(tc.psum_pool(name="h_psum", bufs=3))
         t_psum = ctx.enter_context(tc.psum_pool(name="t_psum", bufs=2))
-        w_psum = ctx.enter_context(tc.psum_pool(name="w_psum", bufs=1))
-        o_psum = ctx.enter_context(tc.psum_pool(name="o_psum", bufs=2))
+        o_psum = ctx.enter_context(tc.psum_pool(name="o_psum", bufs=1))
 
         offsets = keep.tile([P, S // GROUP], U16, name="offsets")
         x_scale_table = keep.tile([P, T], U8, name="x_scale_table", align_bytes=64)
@@ -76,15 +76,17 @@ def tile_picked_haar_gelu_p_kernel(
         nc.sync.dma_start(out=w1_raw[:, LEAD:], in_=w1_rows[:, LEAD:])
         nc.sync.dma_start(out=x_word_table[:], in_=x_words[0].rearrange("p n r -> p (n r)").bitcast(I32))
 
+        band_spread = keep.tile([P, 2 * N], U8, name="band_spread", align_bytes=64)
+        for b, scales in enumerate((w2_scales, w3_scales)):
+            nc.sync.dma_start(
+                out=band_spread[ROW_FIRST : ROW_FIRST + 16 * ROW_STEP : ROW_STEP, b * N : (b + 1) * N].bitcast(I32),
+                in_=scales[0].bitcast(I32),
+            )
+
         for plane, (e0, e1) in zip(picked_scales, pieces):
             spread = keep.tile([P, e1 - e0], U8, name="spread_scales%d" % e0, align_bytes=64)
             nc.vector.tensor_copy(spread[:], x_scale_table[:].indirect(offsets[:, e0 // GROUP : e1 // GROUP]))
-            for r in range(4):
-                row = ROW_FIRST + r * ROW_STEP
-                nc.sync.dma_start(
-                    out=plane[r:P:32, :].bitcast(I32),
-                    in_=spread[row : row + 12 * ROW_STEP + 1 : 4 * ROW_STEP, :].bitcast(I32),
-                )
+            move_scale_rows(nc, plane, spread)
 
         w1_bf16 = early.tile([P, PACK * H], BF16, name="w1_bf16", align_bytes=64, offset=0)
         dealt = w1_bf16[:].rearrange("p (t m j) -> p m j t", t=PACK, j=PACK)
@@ -101,27 +103,25 @@ def tile_picked_haar_gelu_p_kernel(
                 out=w1_codes[:, c0:c1].bitcast(FP8X4), scales=w1_scales[:, c0:c1], in_=w1_bf16[:, PACK * c0 : PACK * c1]
             )
 
-        warm = w_psum.tile([P, 2 * P], F32, name="warm")
+        warm = o_psum.tile([P, 2 * P], F32, name="o_bank%d" % TURNED)
         for rep in range(WARM_UPS):
             nc.tensor.matmul_mx(
                 out=warm[:],
-                lhsT=w1_codes[:, :P].bitcast(FP8X4),
-                lhsT_scale=w1_scales[:, :P],
-                rhs=w1_codes[:, : 2 * P].bitcast(FP8X4),
-                rhs_scale=w1_scales[:, : 2 * P],
+                lhsT=w1_codes[:, 2 * P : 3 * P].bitcast(FP8X4),
+                lhsT_scale=w1_scales[:, 2 * P : 3 * P],
+                rhs=w1_codes[:, 2 * P :].bitcast(FP8X4),
+                rhs_scale=w1_scales[:, 2 * P :],
                 start=True,
                 stop=True,
             )
 
         band_words = []
-        band_scales = []
-        for b, (words, scales) in enumerate(((w2_words, w2_scales), (w3_words, w3_scales))):
-            at = b * 3 * N
-            band_words.append(early.tile([P, 2 * N], U8, name="band_words%d" % b, align_bytes=64, offset=at))
-            band_scales.append(early.tile([P, N], U8, name="band_scales%d" % b, align_bytes=64, offset=at + 2 * N))
-            nc.gpsimd.memset(band_scales[b][:].bitcast(I32), 0)
+        for b, words in enumerate((w2_words, w3_words)):
+            band_words.append(early.tile([P, 2 * N], U8, name="band_words%d" % b, align_bytes=64, offset=b * 2 * N))
             nc.sync.dma_start(out=band_words[b][:].bitcast(I32), in_=words[0].bitcast(I32))
-            load_scale_rows(nc.sync, band_scales[b], scales[0])
+        band_scales = early.tile([P, 2 * N], U8, name="band_scales", align_bytes=64, offset=4 * N)
+        nc.gpsimd.memset(band_scales[:].bitcast(I32), 0)
+        move_scale_rows(nc, band_scales, band_spread)
 
         picked_words = {}
         for e0, e1 in GATHERS:
@@ -217,19 +217,22 @@ def tile_picked_haar_gelu_p_kernel(
             nc.vector.quantize_mx(out=words[:].bitcast(FP8X4), scales=scales[:], in_=bands[b, c][:])
             codes[b, c] = (words, scales)
 
-        def finish(c):
-            acc = o_psum.tile([P, CHUNK], F32, name="o_bank")
+        def second_layer(c, acc):
             for b in range(2):
                 words, scales = codes[b, c]
                 nc.tensor.matmul_mx(
-                    out=acc[:],
+                    out=acc,
                     lhsT=band_words[b][:].bitcast(FP4X4),
-                    lhsT_scale=band_scales[b][:],
+                    lhsT_scale=band_scales[:, b * N : (b + 1) * N],
                     rhs=words[:].bitcast(FP8X4),
                     rhs_scale=scales[:],
                     start=(b == 0),
                     stop=(b == 1),
                 )
+
+        def finish(c):
+            acc = o_psum.tile([P, CHUNK], F32, name="o_bank%d" % c)
+            second_layer(c, acc[:])
             result = keep.tile([P, CHUNK], F32, name="result%d" % c)
             if c == LAST:
                 nc.vector.tensor_scalar_mul(result[:], acc[:], 0.5)
@@ -248,10 +251,14 @@ def tile_picked_haar_gelu_p_kernel(
         quantise_band(1, 1)
         turn_band(0, hidden[1, TURNED])
         turn_band(1, negated)
-        finish(0)
-        finish(1)
+        both = o_psum.tile([P, 2 * CHUNK], F32, name="o_bank_both")
+        for c in range(2):
+            second_layer(c, both[:, c * CHUNK : (c + 1) * CHUNK])
         make_bands_by_halves(3)
         quantise_band(0, TURNED)
+        result = keep.tile([P, 2 * CHUNK], F32, name="band0_%d" % TURNED, align_bytes=64)
+        nc.scalar.activation(out=result[:], in_=both[:], func=COPY, scale=0.5)
+        nc.sync.dma_start(out=out[:, : 2 * CHUNK], in_=result[:])
         quantise_band(0, 3)
         quantise_band(1, 3)
         finish(3)

@@ -133,6 +133,16 @@ def tile_picked_haar_gelu_p_kernel(
                 picked_words[first] = picked[:, first - e0 : first - e0 + CHUNK]
 
         hidden = {}
+        banks = {}
+
+        def gelu(d, c, part, parts):
+            cols = slice(part * CHUNK // parts, (part + 1) * CHUNK // parts)
+            nc.scalar.activation(
+                out=hidden[d, c][:].rearrange("p (n t) -> p n t", t=PACK)[:, cols],
+                in_=banks[d, c][:].rearrange("p t n -> p n t")[:, cols],
+                func=GELU,
+            )
+
         for c in range(CHUNKS):
             for d in range(2):
                 first = d * V + c * CHUNK
@@ -142,6 +152,7 @@ def tile_picked_haar_gelu_p_kernel(
                 bank = h_psum.tile([P, PACK, CHUNK], F32, name="h_bank")
                 h = keep.tile([P, CHUNK * PACK], F32, name="hidden%d_%d" % (d, c), align_bytes=64)
                 hidden[d, c] = h
+                banks[d, c] = bank
                 if c == TURNED:
                     flat = bank[:].rearrange("p t n -> p (t n)")
                     nc.tensor.matmul_mx(
@@ -165,14 +176,13 @@ def tile_picked_haar_gelu_p_kernel(
                         start=True,
                         stop=True,
                     )
-                parts = 2 if d == 1 and c in (0, CHUNKS - 1) else 1
-                for part in range(parts):
-                    cols = slice(part * CHUNK // parts, (part + 1) * CHUNK // parts)
-                    nc.scalar.activation(
-                        out=h[:].rearrange("p (n t) -> p n t", t=PACK)[:, cols],
-                        in_=bank[:].rearrange("p t n -> p n t")[:, cols],
-                        func=GELU,
-                    )
+                if c < CHUNKS - 1:
+                    parts = 2 if (d, c) == (1, 0) else 1
+                    for part in range(parts):
+                        gelu(d, c, part, parts)
+        for part in range(2):
+            for d in range(2):
+                gelu(d, CHUNKS - 1, part, 2)
 
         bands = {}
         codes = {}

@@ -34,6 +34,8 @@ M_SHARED = 32
 TURNED = 2
 LAST = TURNED
 WARM_UPS = 2
+FIRST_CUTS = (0, 32, 64, 128)
+LAST_CUTS = (0, 64, 128)
 
 
 def move_scale_rows(nc, plane, spread):
@@ -67,6 +69,8 @@ def tile_picked_haar_gelu_p_kernel(
         nc.gpsimd.memset(x_scale_table[:].bitcast(I32), 0)
         for plane in picked_scales:
             nc.vector.memset(plane[:].bitcast(I32), 0)
+        band_scales = keep.tile([P, 2 * N], U8, name="band_scales", align_bytes=64)
+        nc.vector.memset(band_scales[:].bitcast(I32), 0)
         make_identity(nc, identity[:])
 
         w1_rows = w1.rearrange("(p j) c -> p (j c)", j=PACK)
@@ -107,10 +111,10 @@ def tile_picked_haar_gelu_p_kernel(
         for rep in range(WARM_UPS):
             nc.tensor.matmul_mx(
                 out=warm[:],
-                lhsT=w1_codes[:, 2 * P : 3 * P].bitcast(FP8X4),
-                lhsT_scale=w1_scales[:, 2 * P : 3 * P],
-                rhs=w1_codes[:, 2 * P :].bitcast(FP8X4),
-                rhs_scale=w1_scales[:, 2 * P :],
+                lhsT=w1_codes[:, :P].bitcast(FP8X4),
+                lhsT_scale=w1_scales[:, :P],
+                rhs=w1_codes[:, : 2 * P].bitcast(FP8X4),
+                rhs_scale=w1_scales[:, : 2 * P],
                 start=True,
                 stop=True,
             )
@@ -119,8 +123,6 @@ def tile_picked_haar_gelu_p_kernel(
         for b, words in enumerate((w2_words, w3_words)):
             band_words.append(early.tile([P, 2 * N], U8, name="band_words%d" % b, align_bytes=64, offset=b * 2 * N))
             nc.sync.dma_start(out=band_words[b][:].bitcast(I32), in_=words[0].bitcast(I32))
-        band_scales = early.tile([P, 2 * N], U8, name="band_scales", align_bytes=64, offset=4 * N)
-        nc.gpsimd.memset(band_scales[:].bitcast(I32), 0)
         move_scale_rows(nc, band_scales, band_spread)
 
         picked_words = {}
@@ -135,8 +137,8 @@ def tile_picked_haar_gelu_p_kernel(
         hidden = {}
         banks = {}
 
-        def gelu(d, c, part, parts):
-            cols = slice(part * CHUNK // parts, (part + 1) * CHUNK // parts)
+        def gelu(d, c, n0, n1):
+            cols = slice(n0, n1)
             nc.scalar.activation(
                 out=hidden[d, c][:].rearrange("p (n t) -> p n t", t=PACK)[:, cols],
                 in_=banks[d, c][:].rearrange("p t n -> p n t")[:, cols],
@@ -177,12 +179,12 @@ def tile_picked_haar_gelu_p_kernel(
                         stop=True,
                     )
                 if c < CHUNKS - 1:
-                    parts = 2 if (d, c) == (1, 0) else 1
-                    for part in range(parts):
-                        gelu(d, c, part, parts)
-        for part in range(2):
+                    cuts = FIRST_CUTS if (d, c) == (1, 0) else (0, CHUNK)
+                    for n0, n1 in zip(cuts, cuts[1:]):
+                        gelu(d, c, n0, n1)
+        for n0, n1 in zip(LAST_CUTS, LAST_CUTS[1:]):
             for d in range(2):
-                gelu(d, CHUNKS - 1, part, 2)
+                gelu(d, CHUNKS - 1, n0, n1)
 
         bands = {}
         codes = {}
@@ -192,12 +194,11 @@ def tile_picked_haar_gelu_p_kernel(
             nc.vector.tensor_tensor(band[:], hidden[0, c][:], hidden[1, c][:], (ADD, SUBTRACT)[b])
             bands[b, c] = band
 
-        def make_bands_by_halves(c):
-            width = CHUNK * PACK // 2
+        def make_bands_in_parts(c, cuts):
             for b in range(2):
                 bands[b, c] = keep.tile([P, CHUNK * PACK], BF16, name="band%d_%d" % (b, c), align_bytes=64)
-            for part in range(2):
-                cols = slice(part * width, (part + 1) * width)
+            for n0, n1 in zip(cuts, cuts[1:]):
+                cols = slice(n0 * PACK, n1 * PACK)
                 for b in range(2):
                     nc.vector.tensor_tensor(
                         bands[b, c][:, cols], hidden[0, c][:, cols], hidden[1, c][:, cols], (ADD, SUBTRACT)[b]
@@ -216,15 +217,22 @@ def tile_picked_haar_gelu_p_kernel(
                         stop=(d, t) == (1, PACK - 1),
                     )
             band = keep.tile([P, CHUNK * PACK], BF16, name="band%d_%d" % (b, TURNED), align_bytes=64)
-            nc.scalar.copy(
-                out=band[:].rearrange("p (n t) -> p n t", t=PACK), in_=bank[:].rearrange("p t n -> p n t")
-            )
+            cuts = LAST_CUTS if b == 1 else (0, CHUNK)
+            for n0, n1 in zip(cuts, cuts[1:]):
+                nc.scalar.copy(
+                    out=band[:].rearrange("p (n t) -> p n t", t=PACK)[:, n0:n1],
+                    in_=bank[:].rearrange("p t n -> p n t")[:, n0:n1],
+                )
             bands[b, TURNED] = band
 
         def quantise_band(b, c):
             words = keep.tile([P, CHUNK], U32, name="band_codes%d_%d" % (b, c), align_bytes=64)
             scales = keep.tile([P, CHUNK], U8, name="band_code_scales%d_%d" % (b, c), align_bytes=64)
-            nc.vector.quantize_mx(out=words[:].bitcast(FP8X4), scales=scales[:], in_=bands[b, c][:])
+            cuts = LAST_CUTS if (b, c) == (1, TURNED) else (0, CHUNK)
+            for n0, n1 in zip(cuts, cuts[1:]):
+                nc.vector.quantize_mx(
+                    out=words[:, n0:n1].bitcast(FP8X4), scales=scales[:, n0:n1], in_=bands[b, c][:, n0 * PACK : n1 * PACK]
+                )
             codes[b, c] = (words, scales)
 
         def second_layer(c, acc):
@@ -250,7 +258,7 @@ def tile_picked_haar_gelu_p_kernel(
                 nc.scalar.activation(out=result[:], in_=acc[:], func=COPY, scale=0.5)
             nc.sync.dma_start(out=out[:, c * CHUNK : (c + 1) * CHUNK], in_=result[:])
 
-        make_bands_by_halves(0)
+        make_bands_in_parts(0, FIRST_CUTS)
         quantise_band(0, 0)
         make_band(0, 1)
         quantise_band(1, 0)
@@ -264,7 +272,7 @@ def tile_picked_haar_gelu_p_kernel(
         both = o_psum.tile([P, 2 * CHUNK], F32, name="o_bank_both")
         for c in range(2):
             second_layer(c, both[:, c * CHUNK : (c + 1) * CHUNK])
-        make_bands_by_halves(3)
+        make_bands_in_parts(3, LAST_CUTS)
         quantise_band(0, TURNED)
         result = keep.tile([P, 2 * CHUNK], F32, name="band0_%d" % TURNED, align_bytes=64)
         nc.scalar.activation(out=result[:], in_=both[:], func=COPY, scale=0.5)

@@ -27,7 +27,7 @@ CHUNKS = V // CHUNK
 GATHERS = ((0, 128), (512, 768), (128, 384), (768, 1024), (384, 512))
 LATE = 256
 ROW_FIRST, ROW_STEP = 11, 7
-LEAD = 512
+LEAD = 768
 T_SCALAR = 2
 M_EARLY = 8
 M_SHARED = 32
@@ -151,7 +151,10 @@ def tile_picked_haar_gelu_p_kernel(
                 tokens = picked_words[first].bitcast(FP8X4)
                 piece, at = divmod(first, S - LATE)
                 token_scales = picked_scales[piece][:, at : at + CHUNK]
-                bank = h_psum.tile([P, PACK, CHUNK], F32, name="h_bank")
+                if (d, c) == (1, CHUNKS - 1):
+                    bank = o_psum.tile([P, PACK, CHUNK], F32, name="o_bank%d" % TURNED)
+                else:
+                    bank = h_psum.tile([P, PACK, CHUNK], F32, name="h_bank")
                 h = keep.tile([P, CHUNK * PACK], F32, name="hidden%d_%d" % (d, c), align_bytes=64)
                 hidden[d, c] = h
                 banks[d, c] = bank

@@ -33,7 +33,6 @@ M_EARLY = 8
 M_SHARED = 32
 TURNED = 2
 LAST = TURNED
-WARM_UPS = 2
 FIRST_CUTS = (0, 32, 64, 128)
 LAST_CUTS = (0, 64, 128)
 
@@ -105,18 +104,6 @@ def tile_picked_haar_gelu_p_kernel(
         for c0, c1 in ((0, T_SCALAR * P), (T_SCALAR * P, H)):
             nc.vector.quantize_mx(
                 out=w1_codes[:, c0:c1].bitcast(FP8X4), scales=w1_scales[:, c0:c1], in_=w1_bf16[:, PACK * c0 : PACK * c1]
-            )
-
-        warm = o_psum.tile([P, 2 * P], F32, name="o_bank%d" % TURNED)
-        for rep in range(WARM_UPS):
-            nc.tensor.matmul_mx(
-                out=warm[:],
-                lhsT=w1_codes[:, :P].bitcast(FP8X4),
-                lhsT_scale=w1_scales[:, :P],
-                rhs=w1_codes[:, : 2 * P].bitcast(FP8X4),
-                rhs_scale=w1_scales[:, : 2 * P],
-                start=True,
-                stop=True,
             )
 
         band_words = []

from contextlib import ExitStack

import concourse.mybir as mybir
from concourse.masks import make_identity

K, T, S, V, H, N = 512, 2048, 1024, 512, 512, 128
FLOPS = 2 * K * H * S + 2 * 2 * H * N * V

F32 = mybir.dt.float32
BF16 = mybir.dt.bfloat16
I32 = mybir.dt.int32
U32 = mybir.dt.uint32
U16 = mybir.dt.uint16
U8 = mybir.dt.uint8
FP8X4 = mybir.dt.float8_e4m3fn_x4
FP4X4 = mybir.dt.float4_e2m1fn_x4
GELU = mybir.ActivationFunctionType.Gelu_apprx_tanh
COPY = mybir.ActivationFunctionType.Copy
ADD = mybir.AluOpType.add
SUBTRACT = mybir.AluOpType.subtract

P = 128
PACK = 4
GROUP = 16
CHUNK = 128
CHUNKS = V // CHUNK
GATHERS = ((0, 128), (512, 768), (128, 384), (768, 1024), (384, 512))
LATE = 256
ROW_FIRST, ROW_STEP = 11, 7
LEAD = 768
T_SCALAR = 2
M_EARLY = 8
M_SHARED = 32
TURNED = 2
LAST = TURNED
FIRST_CUTS = (0, 32, 64, 128)
LAST_CUTS = (0, 64, 128)


def move_scale_rows(nc, plane, spread):
    for r in range(4):
        row = ROW_FIRST + r * ROW_STEP
        nc.sync.dma_start(
            out=plane[r:P:32, :].bitcast(I32),
            in_=spread[row : row + 12 * ROW_STEP + 1 : 4 * ROW_STEP, :].bitcast(I32),
        )


def tile_picked_haar_gelu_p_kernel(
    tc, x_words, x_scales, w1, w2_words, w2_scales, w3_words, w3_scales, offs, out
):
    nc = tc.nc
    with ExitStack() as ctx:
        keep = ctx.enter_context(tc.tile_pool(name="keep", bufs=1))
        early = ctx.enter_context(tc.tile_pool(name="early", bufs=1))
        h_psum = ctx.enter_context(tc.psum_pool(name="h_psum", bufs=3))
        t_psum = ctx.enter_context(tc.psum_pool(name="t_psum", bufs=2))
        o_psum = ctx.enter_context(tc.psum_pool(name="o_psum", bufs=1))

        offsets = keep.tile([P, S // GROUP], U16, name="offsets")
        x_scale_table = keep.tile([P, T], U8, name="x_scale_table", align_bytes=64)
        pieces = ((0, S - LATE), (S - LATE, S))
        picked_scales = [keep.tile([P, e1 - e0], U8, name="picked_scales%d" % e0, align_bytes=64) for e0, e1 in pieces]
        x_word_table = keep.tile([P, T], I32, name="x_word_table", align_bytes=64)
        w1_raw = keep.tile([P, PACK * H], F32, name="w1_raw", align_bytes=64)
        identity = keep.tile([P, P], F32, name="identity", align_bytes=64)

        nc.gpsimd.memset(x_scale_table[:].bitcast(I32), 0)
        for plane in picked_scales:
            nc.vector.memset(plane[:].bitcast(I32), 0)
        band_scales = keep.tile([P, 2 * N], U8, name="band_scales", align_bytes=64)
        nc.vector.memset(band_scales[:].bitcast(I32), 0)
        make_identity(nc, identity[:])

        w1_rows = w1.rearrange("(p j) c -> p (j c)", j=PACK)
        nc.sync.dma_start(out=w1_raw[:, :LEAD], in_=w1_rows[:, :LEAD])
        nc.sync.dma_start(offsets[:], offs)
        nc.sync.dma_start(out=x_scale_table[ROW_FIRST : ROW_FIRST + 16 * ROW_STEP : ROW_STEP, :].bitcast(I32), in_=x_scales[0].bitcast(I32))
        nc.sync.dma_start(out=w1_raw[:, LEAD:], in_=w1_rows[:, LEAD:])
        nc.sync.dma_start(out=x_word_table[:], in_=x_words[0].rearrange("p n r -> p (n r)").bitcast(I32))

        band_spread = keep.tile([P, 2 * N], U8, name="band_spread", align_bytes=64)
        for b, scales in enumerate((w2_scales, w3_scales)):
            nc.sync.dma_start(
                out=band_spread[ROW_FIRST : ROW_FIRST + 16 * ROW_STEP : ROW_STEP, b * N : (b + 1) * N].bitcast(I32),
                in_=scales[0].bitcast(I32),
            )

        for plane, (e0, e1) in zip(picked_scales, pieces):
            spread = keep.tile([P, e1 - e0], U8, name="spread_scales%d" % e0, align_bytes=64)
            nc.vector.tensor_copy(spread[:], x_scale_table[:].indirect(offsets[:, e0 // GROUP : e1 // GROUP]))
            move_scale_rows(nc, plane, spread)

        w1_bf16 = early.tile([P, PACK * H], BF16, name="w1_bf16", align_bytes=64, offset=0)
        dealt = w1_bf16[:].rearrange("p (t m j) -> p m j t", t=PACK, j=PACK)
        undealt = w1_raw[:].rearrange("p (j m t) -> p m j t", j=PACK, t=PACK)
        nc.scalar.copy(out=dealt[:, :M_EARLY, :1, :T_SCALAR], in_=undealt[:, :M_EARLY, :1, :T_SCALAR])
        nc.scalar.copy(out=dealt[:, :M_EARLY, 1:, :T_SCALAR], in_=undealt[:, :M_EARLY, 1:, :T_SCALAR])
        nc.scalar.copy(out=dealt[:, M_EARLY:, :, :T_SCALAR], in_=undealt[:, M_EARLY:, :, :T_SCALAR])
        nc.scalar.copy(out=dealt[:, :M_SHARED, :, T_SCALAR:], in_=undealt[:, :M_SHARED, :, T_SCALAR:])
        nc.vector.tensor_copy(out=dealt[:, M_SHARED:, :, T_SCALAR:], in_=undealt[:, M_SHARED:, :, T_SCALAR:])
        w1_codes = keep.tile([P, H], U32, name="w1_codes", align_bytes=64)
        w1_scales = keep.tile([P, H], U8, name="w1_scales", align_bytes=64)
        for c0, c1 in ((0, T_SCALAR * P), (T_SCALAR * P, H)):
            nc.vector.quantize_mx(
                out=w1_codes[:, c0:c1].bitcast(FP8X4), scales=w1_scales[:, c0:c1], in_=w1_bf16[:, PACK * c0 : PACK * c1]
            )

        band_words = []
        for b, words in enumerate((w2_words, w3_words)):
            band_words.append(early.tile([P, 2 * N], U8, name="band_words%d" % b, align_bytes=64, offset=b * 2 * N))
            nc.sync.dma_start(out=band_words[b][:].bitcast(I32), in_=words[0].bitcast(I32))
        move_scale_rows(nc, band_scales, band_spread)

        picked_words = {}
        for e0, e1 in GATHERS:
            picked = keep.tile([P, e1 - e0], U32, name="picked_words%d" % e0, align_bytes=64)
            nc.vector.tensor_copy(
                picked[:], x_word_table[:].bitcast(U32).indirect(offsets[:, e0 // GROUP : e1 // GROUP])
            )
            for first in range(e0, e1, CHUNK):
                picked_words[first] = picked[:, first - e0 : first - e0 + CHUNK]

        hidden = {}
        banks = {}

        def gelu(d, c, n0, n1):
            cols = slice(n0, n1)
            nc.scalar.activation(
                out=hidden[d, c][:].rearrange("p (n t) -> p n t", t=PACK)[:, cols],
                in_=banks[d, c][:].rearrange("p t n -> p n t")[:, cols],
                func=GELU,
            )

        for c in range(CHUNKS):
            for d in range(2):
                first = d * V + c * CHUNK
                tokens = picked_words[first].bitcast(FP8X4)
                piece, at = divmod(first, S - LATE)
                token_scales = picked_scales[piece][:, at : at + CHUNK]
                if (d, c) == (1, CHUNKS - 1):
                    bank = o_psum.tile([P, PACK, CHUNK], F32, name="o_bank%d" % TURNED)
                else:
                    bank = h_psum.tile([P, PACK, CHUNK], F32, name="h_bank")
                h = keep.tile([P, CHUNK * PACK], F32, name="hidden%d_%d" % (d, c), align_bytes=64)
                hidden[d, c] = h
                banks[d, c] = bank
                if c == TURNED:
                    flat = bank[:].rearrange("p t n -> p (t n)")
                    nc.tensor.matmul_mx(
                        out=flat,
                        lhsT=tokens,
                        lhsT_scale=token_scales,
                        rhs=w1_codes[:].bitcast(FP8X4),
                        rhs_scale=w1_scales[:],
                        start=True,
                        stop=True,
                    )
                    nc.scalar.activation(out=h[:], in_=flat, func=GELU)
                    continue
                for t in range(PACK):
                    nc.tensor.matmul_mx(
                        out=bank[:, t, :],
                        lhsT=w1_codes[:, t * P : (t + 1) * P].bitcast(FP8X4),
                        lhsT_scale=w1_scales[:, t * P : (t + 1) * P],
                        rhs=tokens,
                        rhs_scale=token_scales,
                        start=True,
                        stop=True,
                    )
                if c < CHUNKS - 1:
                    cuts = FIRST_CUTS if (d, c) == (1, 0) else (0, CHUNK)
                    for n0, n1 in zip(cuts, cuts[1:]):
                        gelu(d, c, n0, n1)
        for n0, n1 in zip(LAST_CUTS, LAST_CUTS[1:]):
            for d in range(2):
                gelu(d, CHUNKS - 1, n0, n1)

        bands = {}
        codes = {}

        def make_band(b, c):
            band = keep.tile([P, CHUNK * PACK], BF16, name="band%d_%d" % (b, c), align_bytes=64)
            nc.vector.tensor_tensor(band[:], hidden[0, c][:], hidden[1, c][:], (ADD, SUBTRACT)[b])
            bands[b, c] = band

        def make_bands_in_parts(c, cuts):
            for b in range(2):
                bands[b, c] = keep.tile([P, CHUNK * PACK], BF16, name="band%d_%d" % (b, c), align_bytes=64)
            for n0, n1 in zip(cuts, cuts[1:]):
                cols = slice(n0 * PACK, n1 * PACK)
                for b in range(2):
                    nc.vector.tensor_tensor(
                        bands[b, c][:, cols], hidden[0, c][:, cols], hidden[1, c][:, cols], (ADD, SUBTRACT)[b]
                    )

        def turn_band(b, second):
            bank = t_psum.tile([P, PACK, CHUNK], F32, name="t_bank")
            for d, member in enumerate((hidden[0, TURNED], second)):
                for t in range(PACK):
                    nc.tensor.matmul(
                        out=bank[:, t, :],
                        lhsT=member[:, t * P : (t + 1) * P],
                        rhs=identity[:],
                        is_transpose=True,
                        start=(d, t) == (0, 0),
                        stop=(d, t) == (1, PACK - 1),
                    )
            band = keep.tile([P, CHUNK * PACK], BF16, name="band%d_%d" % (b, TURNED), align_bytes=64)
            cuts = LAST_CUTS if b == 1 else (0, CHUNK)
            for n0, n1 in zip(cuts, cuts[1:]):
                nc.scalar.copy(
                    out=band[:].rearrange("p (n t) -> p n t", t=PACK)[:, n0:n1],
                    in_=bank[:].rearrange("p t n -> p n t")[:, n0:n1],
                )
            bands[b, TURNED] = band

        def quantise_band(b, c):
            words = keep.tile([P, CHUNK], U32, name="band_codes%d_%d" % (b, c), align_bytes=64)
            scales = keep.tile([P, CHUNK], U8, name="band_code_scales%d_%d" % (b, c), align_bytes=64)
            cuts = LAST_CUTS if (b, c) == (1, TURNED) else (0, CHUNK)
            for n0, n1 in zip(cuts, cuts[1:]):
                nc.vector.quantize_mx(
                    out=words[:, n0:n1].bitcast(FP8X4), scales=scales[:, n0:n1], in_=bands[b, c][:, n0 * PACK : n1 * PACK]
                )
            codes[b, c] = (words, scales)

        def second_layer(c, acc):
            for b in range(2):
                words, scales = codes[b, c]
                nc.tensor.matmul_mx(
                    out=acc,
                    lhsT=band_words[b][:].bitcast(FP4X4),
                    lhsT_scale=band_scales[:, b * N : (b + 1) * N],
                    rhs=words[:].bitcast(FP8X4),
                    rhs_scale=scales[:],
                    start=(b == 0),
                    stop=(b == 1),
                )

        def finish(c):
            acc = o_psum.tile([P, CHUNK], F32, name="o_bank%d" % c)
            second_layer(c, acc[:])
            result = keep.tile([P, CHUNK], F32, name="result%d" % c)
            if c == LAST:
                nc.vector.tensor_scalar_mul(result[:], acc[:], 0.5)
            else:
                nc.scalar.activation(out=result[:], in_=acc[:], func=COPY, scale=0.5)
            nc.sync.dma_start(out=out[:, c * CHUNK : (c + 1) * CHUNK], in_=result[:])

        make_bands_in_parts(0, FIRST_CUTS)
        quantise_band(0, 0)
        make_band(0, 1)
        quantise_band(1, 0)
        make_band(1, 1)
        quantise_band(0, 1)
        negated = keep.tile([P, CHUNK * PACK], F32, name="negated", align_bytes=64)
        nc.vector.tensor_scalar_mul(negated[:], hidden[1, TURNED][:], -1.0)
        quantise_band(1, 1)
        turn_band(0, hidden[1, TURNED])
        turn_band(1, negated)
        both = o_psum.tile([P, 2 * CHUNK], F32, name="o_bank_both")
        for c in range(2):
            second_layer(c, both[:, c * CHUNK : (c + 1) * CHUNK])
        make_bands_in_parts(3, LAST_CUTS)
        quantise_band(0, TURNED)
        result = keep.tile([P, 2 * CHUNK], F32, name="band0_%d" % TURNED, align_bytes=64)
        nc.scalar.activation(out=result[:], in_=both[:], func=COPY, scale=0.5)
        nc.sync.dma_start(out=out[:, : 2 * CHUNK], in_=result[:])
        quantise_band(0, 3)
        quantise_band(1, 3)
        finish(3)
        quantise_band(1, TURNED)
        finish(TURNED)
